import numpy as np
import ml_dtypes


def mxq(x, axis, fmt="e4m3"):
    dtype, down = {"e4m3": (ml_dtypes.float8_e4m3fn, 7), "e5m2": (ml_dtypes.float8_e5m2, 14)}[fmt]
    v = np.moveaxis(np.asarray(x, np.float32).astype(ml_dtypes.bfloat16).astype(np.float64), axis, -1)
    blocks = v.reshape(v.shape[:-1] + (-1, 32))
    amax = np.abs(blocks).max(-1, keepdims=True)
    byte = np.maximum(np.where(amax > 0, np.frexp(amax)[1] - 1 + 127, 0) - down, 1)
    scale = np.exp2(byte - 127.0)
    codes = (blocks / scale).astype(np.float32).astype(dtype).astype(np.float64)
    return np.moveaxis((codes * scale).reshape(v.shape), -1, axis)


WIDE = False


def mx_kscale(k):
    if not WIDE:
        return np.ones(k)
    levels = np.array([10, -10, 5, -5, 0])
    if k % 512:
        return np.exp2(np.random.permutation(np.resize(levels, k // 32))).repeat(32)
    a = np.empty((k // 512, 16))
    for p in range(k // 512):
        a[p, :8] = np.random.permutation(np.resize(levels, 8))
        for g in range(8):
            far = levels[np.abs(levels - a[p, g]) >= 10]
            a[p, g + 8] = far[np.random.randint(len(far))]
    return np.exp2(a.ravel()).repeat(32)


def f64(x):
    return np.asarray(x).astype(np.float64)


def striped(idx):
    return np.tile(idx.reshape(-1, 16).T, (8, 1)).astype(np.uint16)


def unstriped(offs):
    return offs[:16].T.reshape(-1).astype(np.int64)


def relu2(v):
    return np.maximum(v, 0.0) ** 2


K, T, S, H, N = 1024, 2048, 768, 512, 512


def setup_inputs():
    n = np.random.standard_normal
    s = mx_kscale(K)[:, None]
    u = mx_kscale(H)
    return {
        "xT": (n((K, T)) * s).astype(np.float32),
        "w1": (n((K, H)) / np.sqrt(K) / s * u).astype(np.float32),
        "w2": (n((H, N)) / np.sqrt(H) / u[:, None] ** 2).astype(np.float32),
        "offs": striped(np.sort(np.random.permutation(T)[:S])),
    }


def reference(xT, w1, w2, offs):
    idx = unstriped(offs)
    xq = mxq(f64(xT)[:, idx], 0, "e4m3")
    h = relu2(mxq(f64(w1), 0, "e4m3").T @ xq)
    y = mxq(f64(w2), 0, "e4m3").T @ mxq(h, 0, "e4m3")
    return y

@@ -1,0 +1,273 @@
+from contextlib import ExitStack
+
+import concourse.mybir as mybir
+
+K, T, S, H, N = 1024, 2048, 768, 512, 512
+FLOPS = 2 * S * (K * H + H * N)
+
+F32 = mybir.dt.float32
+BF16 = mybir.dt.bfloat16
+U32 = mybir.dt.uint32
+U16 = mybir.dt.uint16
+U8 = mybir.dt.uint8
+FP8X4 = mybir.dt.float8_e4m3fn_x4
+RELU = mybir.ActivationFunctionType.Relu
+SQUARE = mybir.ActivationFunctionType.Square
+MULT = mybir.AluOpType.mult
+
+P = 128
+CH = 256
+CHUNKS = S // CH
+HEAD = T - S + CH
+
+
+def tile_picked_pick_mlp_relu2_srt_e_kernel(tc, xT, w1, w2, offs, out):
+    nc = tc.nc
+    with ExitStack() as ctx:
+        keep = ctx.enter_context(tc.tile_pool(name="keep", bufs=1))
+        turns = ctx.enter_context(tc.tile_pool(name="turns", bufs=1))
+        psum = ctx.enter_context(tc.psum_pool(name="psum", bufs=8))
+
+        x_view = xT.rearrange("(s p j) t -> s j p t", s=2, j=4)
+        w1_view = w1.rearrange("(s p j) c -> s p j c", s=2, j=4)
+        w2_view = w2.rearrange("(p j) c -> p j c", j=4)
+        out_view = out.rearrange("(b i p) n -> b p i n", b=2, i=2)
+
+        offsets = keep.tile([P, S // 16], U16, name="offsets")
+        x = [[keep.tile([P, T], F32, name="x%d%d" % (s, j)) for j in range(4)] for s in range(2)]
+        w1_raw = [keep.tile([P, 4, H], F32, name="w1_raw%d" % s) for s in range(2)]
+        w2_raw = keep.tile([P, 4, N], F32, name="w2_raw")
+
+        def load_x(s, j):
+            nc.sync.dma_start(x[s][j][:], x_view[s, j])
+
+        def load_w1(s):
+            nc.sync.dma_start(w1_raw[s][:], w1_view[s])
+
+        load_x(0, 0)
+        nc.sync.dma_start(offsets[:], offs)
+        load_x(0, 1)
+        load_w1(0)
+        load_x(0, 2)
+        load_x(0, 3)
+        load_x(1, 0)
+        load_w1(1)
+        load_x(1, 1)
+        load_x(1, 2)
+        for cols in (slice(0, HEAD), slice(HEAD, T)):
+            nc.sync.dma_start(x[1][3][:, cols], x_view[1, 3][:, cols])
+        nc.sync.dma_start(w2_raw[:], w2_view)
+
+        picked = [keep.tile([P, 4, S], F32, name="picked%d" % s) for s in range(2)]
+        x_bf = [
+            keep.tile([P, S, 4], BF16, name="x_bf0", align_bytes=64),
+            turns.tile([P, S, 4], BF16, name="x_bf1", tag="bf", align_bytes=64),
+        ]
+        x_codes = [keep.tile([P, S], U32, name="x_codes%d" % s, align_bytes=64) for s in range(2)]
+        x_scales = [keep.tile([P, S], U8, name="x_scales%d" % s, align_bytes=64) for s in range(2)]
+        w1_bf = [keep.tile([P, 4 * H], BF16, name="w1_bf%d" % s, align_bytes=64) for s in range(2)]
+        w1_codes = [keep.tile([P, H], U32, name="w1_codes%d" % s, align_bytes=64) for s in range(2)]
+        w1_scales = [keep.tile([P, H], U8, name="w1_scales%d" % s, align_bytes=64) for s in range(2)]
+        w2_codes = keep.tile([P, N], U32, name="w2_codes", align_bytes=64)
+        w2_scales = keep.tile([P, N], U8, name="w2_scales", align_bytes=64)
+        r = [keep.tile([P, 4, n], F32, name="r%d" % n) for n in (CH, S - CH)]
+        h_bf = [keep.tile([P, CH, 4], BF16, name="h_bf%d" % c, align_bytes=64) for c in range(CHUNKS)]
+        h_codes = [keep.tile([P, CH], U32, name="h_codes%d" % c, align_bytes=64) for c in range(CHUNKS)]
+        h_scales = [keep.tile([P, CH], U8, name="h_scales%d" % c, align_bytes=64) for c in range(CHUNKS)]
+        y = [[keep.tile([P, 2, CH], F32, name="y%d%d" % (c, b)) for b in range(2)] for c in range(CHUNKS)]
+
+        def chunk(c):
+            return slice(CH * c, CH * (c + 1))
+
+        def interleave(copy, dst, src):
+            copy(
+                out=dst.rearrange("p (c i) t -> p c t i", i=4),
+                in_=src.rearrange("p t (c i) -> p c t i", i=4),
+            )
+
+        def quantize(codes, scales, values):
+            nc.vector.quantize_mx(out=codes.bitcast(FP8X4), scales=scales, in_=values)
+
+        def gather(s, j):
+            nc.vector.tensor_copy(picked[s][:, j, :], x[s][j][:].indirect(offsets[:]))
+
+        def gather_part(first, last, width):
+            nc.vector.tensor_copy(
+                picked[1][:, 3, first:last],
+                x[1][3][:, 0:width].indirect(offsets[:, first // 16 : last // 16]),
+            )
+
+        def x_interleave(copy, s, c):
+            interleave(copy, x_bf[s][:, chunk(c), :], picked[s][:, :, chunk(c)])
+
+        def x_quantize(s, c):
+            quantize(
+                x_codes[s][:, chunk(c)],
+                x_scales[s][:, chunk(c)],
+                x_bf[s][:, chunk(c), :].rearrange("p n t -> p (n t)"),
+            )
+
+        def w1_interleave(copy, s, half):
+            tiles = slice(2 * half, 2 * half + 2)
+            copy(
+                out=w1_bf[s][:].rearrange("p (t m j) -> p m t j", t=4, j=4)[:, :, tiles, :],
+                in_=w1_raw[s][:].rearrange("p j (m t) -> p m t j", t=4)[:, :, tiles, :],
+            )
+
+        def w1_quantize(s):
+            quantize(w1_codes[s][:], w1_scales[s][:], w1_bf[s][:])
+
+        w2_bf_tile = []
+
+        def w2_interleave(copy, q):
+            w2_bf = w2_bf_tile[0]
+            n = slice(P * q, P * (q + 1))
+            interleave(copy, w2_bf[:, n, :], w2_raw[:, :, n])
+
+        def w2_quantize(half):
+            w2_bf = w2_bf_tile[0]
+            n = slice(N // 2 * half, N // 2 * (half + 1))
+            quantize(w2_codes[:, n], w2_scales[:, n], w2_bf[:, n, :].rearrange("p n t -> p (n t)"))
+
+        group_cols = [slice(0, CH), slice(CH, S)]
+        banks = [[], []]
+
+        def mm1(g, s, t):
+            cols = group_cols[g]
+            width = cols.stop - cols.start
+            if s == 0:
+                bank = psum.tile([P, 512], F32, name="bank")
+                banks[g].append(bank)
+            block = slice(P * t, P * (t + 1))
+            nc.tensor.matmul_mx(
+                out=banks[g][t][:, 0:width],
+                lhsT=w1_codes[s][:, block].bitcast(FP8X4),
+                lhsT_scale=w1_scales[s][:, block],
+                rhs=x_codes[s][:, cols].bitcast(FP8X4),
+                rhs_scale=x_scales[s][:, cols],
+                start=(s == 0),
+                stop=(s == 1),
+            )
+
+        def relu_scalar(g, t):
+            width = r[g].shape[2]
+            nc.scalar.activation(r[g][:, t, :], banks[g][t][:, 0:width], RELU)
+
+        def relu_vector(g, t):
+            width = r[g].shape[2]
+            nc.vector.tensor_scalar_max(r[g][:, t, :], banks[g][t][:, 0:width], 0.0)
+
+        def square_views(c, half):
+            g = 0 if c == 0 else 1
+            first = CH * c - group_cols[g].start + CH // 2 * half
+            src = r[g][:, :, first : first + CH // 2].rearrange("p t (c i) -> p c t i", i=4)
+            n = slice(CH // 2 * half, CH // 2 * (half + 1))
+            return h_bf[c][:, n, :].rearrange("p (c i) t -> p c t i", i=4), src
+
+        def square_scalar(c, half):
+            dst, src = square_views(c, half)
+            nc.scalar.activation(dst, src, SQUARE)
+
+        def square_vector(c, half):
+            dst, src = square_views(c, half)
+            nc.vector.tensor_tensor(dst, src, src, MULT)
+
+        def h_quantize(c):
+            quantize(h_codes[c][:], h_scales[c][:], h_bf[c][:].rearrange("p n t -> p (n t)"))
+
+        y_banks = {}
+
+        def mm2(c, b):
+            bank = psum.tile([P, 512], F32, name="bank")
+            for i in range(2):
+                block = slice(P * (2 * b + i), P * (2 * b + i + 1))
+                nc.tensor.matmul_mx(
+                    out=bank[:, CH * i : CH * (i + 1)],
+                    lhsT=w2_codes[:, block].bitcast(FP8X4),
+                    lhsT_scale=w2_scales[:, block],
+                    rhs=h_codes[c][:].bitcast(FP8X4),
+                    rhs_scale=h_scales[c][:],
+                    start=True,
+                    stop=True,
+                )
+            y_banks[c, b] = bank
+
+        def store(copy, c, b):
+            copy(out=y[c][b][:].rearrange("p i n -> p (i n)"), in_=y_banks[c, b][:])
+            nc.sync.dma_start(out_view[b][:, :, chunk(c)], y[c][b][:])
+
+        on_scalar = nc.scalar.copy
+        on_vector = nc.vector.tensor_copy
+
+        gather(0, 0)
+        w1_interleave(on_scalar, 0, 0)
+        w1_interleave(on_scalar, 0, 1)
+        gather(0, 1)
+        w1_quantize(0)
+        gather(0, 2)
+        gather(0, 3)
+        x_interleave(on_scalar, 0, 0)
+        x_interleave(on_vector, 0, 1)
+        x_interleave(on_scalar, 0, 2)
+        gather(1, 0)
+        x_quantize(0, 0)
+        x_quantize(0, 1)
+        w1_interleave(on_scalar, 1, 0)
+        w1_interleave(on_scalar, 1, 1)
+        gather(1, 1)
+        for t in range(4):
+            mm1(0, 0, t)
+        x_quantize(0, 2)
+        for t in range(4):
+            mm1(1, 0, t)
+        w1_quantize(1)
+        gather(1, 2)
+
+        gather_part(0, CH, HEAD)
+        gather_part(CH, S, T)
+        x_interleave(on_scalar, 1, 0)
+        x_interleave(on_scalar, 1, 1)
+        x_interleave(on_vector, 1, 2)
+        for c in range(CHUNKS):
+            x_quantize(1, c)
+        for t in range(4):
+            mm1(0, 1, t)
+        relu_scalar(0, 0)
+        relu_vector(0, 1)
+        relu_scalar(0, 2)
+        relu_scalar(0, 3)
+        for t in range(4):
+            mm1(1, 1, t)
+        w2_bf = turns.tile([P, N, 4], BF16, name="w2_bf", tag="bf", align_bytes=64)
+        w2_bf_tile.append(w2_bf)
+        w2_interleave(on_vector, 2)
+        w2_interleave(on_vector, 1)
+        w2_interleave(on_scalar, 0)
+        w2_quantize(0)
+        relu_scalar(1, 0)
+        square_scalar(0, 0)
+        square_vector(0, 1)
+        relu_vector(1, 1)
+        relu_scalar(1, 2)
+        relu_vector(1, 3)
+        h_quantize(0)
+        w2_interleave(on_scalar, 3)
+        w2_quantize(1)
+        square_vector(1, 0)
+        square_scalar(1, 1)
+        h_quantize(1)
+        square_vector(2, 0)
+        square_scalar(2, 1)
+        mm2(0, 0)
+        mm2(0, 1)
+        store(on_scalar, 0, 0)
+        store(on_scalar, 0, 1)
+        mm2(1, 0)
+        mm2(1, 1)
+        h_quantize(2)
+        store(on_vector, 1, 0)
+        store(on_scalar, 1, 1)
+        mm2(2, 0)
+        mm2(2, 1)
+        store(on_scalar, 2, 0)
+        store(on_vector, 2, 1)

@@ -25,56 +25,55 @@ def tile_picked_pick_mlp_relu2_srt_e_kernel(tc, xT, w1, w2, offs, out):
     nc = tc.nc
     with ExitStack() as ctx:
         keep = ctx.enter_context(tc.tile_pool(name="keep", bufs=1))
-        turns = ctx.enter_context(tc.tile_pool(name="turns", bufs=1))
         psum = ctx.enter_context(tc.psum_pool(name="psum", bufs=8))
 
         x_view = xT.rearrange("(s p j) t -> s j p t", s=2, j=4)
         w1_view = w1.rearrange("(s p j) c -> s p j c", s=2, j=4)
-        w2_view = w2.rearrange("(p j) c -> p j c", j=4)
+        w2_view = w2.rearrange("(p j) (b c) -> b p j c", j=4, b=2)
         out_view = out.rearrange("(b i p) n -> b p i n", b=2, i=2)
 
         offsets = keep.tile([P, S // 16], U16, name="offsets")
         x = [[keep.tile([P, T], F32, name="x%d%d" % (s, j)) for j in range(4)] for s in range(2)]
         w1_raw = [keep.tile([P, 4, H], F32, name="w1_raw%d" % s) for s in range(2)]
-        w2_raw = keep.tile([P, 4, N], F32, name="w2_raw")
+        w2_raw = [keep.tile([P, 4, N // 2], F32, name="w2_raw%d" % b) for b in range(2)]
 
-        def load_x(s, j):
-            nc.sync.dma_start(x[s][j][:], x_view[s, j])
-
-        def load_w1(s):
-            nc.sync.dma_start(w1_raw[s][:], w1_view[s])
-
-        load_x(0, 0)
+        nc.sync.dma_start(x[0][0][:], x_view[0, 0])
         nc.sync.dma_start(offsets[:], offs)
-        load_x(0, 1)
-        load_w1(0)
-        load_x(0, 2)
-        load_x(0, 3)
-        load_x(1, 0)
-        load_w1(1)
-        load_x(1, 1)
-        load_x(1, 2)
+        for s, j in [(0, 1), (0, 2), (0, 3), (1, 0), (1, 1), (1, 2)]:
+            nc.sync.dma_start(x[s][j][:], x_view[s, j])
         for cols in (slice(0, HEAD), slice(HEAD, T)):
             nc.sync.dma_start(x[1][3][:, cols], x_view[1, 3][:, cols])
-        nc.sync.dma_start(w2_raw[:], w2_view)
+        for s in range(2):
+            nc.sync.dma_start(w1_raw[s][:], w1_view[s])
+        for b in range(2):
+            nc.sync.dma_start(w2_raw[b][:], w2_view[b])
 
-        picked = [keep.tile([P, 4, S], F32, name="picked%d" % s) for s in range(2)]
-        x_bf = [
-            keep.tile([P, S, 4], BF16, name="x_bf0", align_bytes=64),
-            turns.tile([P, S, 4], BF16, name="x_bf1", tag="bf", align_bytes=64),
+        def tiles(name, shape, dtype, *counts):
+            if len(counts) == 1:
+                return [keep.tile(shape, dtype, name="%s_%d" % (name, a), align_bytes=64) for a in range(counts[0])]
+            return [tiles("%s_%d" % (name, a), shape, dtype, *counts[1:]) for a in range(counts[0])]
+
+        picked = tiles("picked", [P, 4, S], F32, 2)
+        x_bf = tiles("x_bf", [P, CH, 4], BF16, 2, CHUNKS)
+        x_codes = [tiles("x_codes_first", [P, CH], U32, 2), tiles("x_codes_rest", [P, S - CH], U32, 1)]
+        x_scales = [tiles("x_scales_first", [P, CH], U8, 2), tiles("x_scales_rest", [P, S - CH], U8, 2)]
+        w1_bf = [
+            [
+                keep.tile([P, 2 * P, 4], BF16, name="w1_bf00", tag="shared", align_bytes=64),
+                keep.tile([P, 2 * P, 4], BF16, name="w1_bf01", align_bytes=64),
+            ],
+            tiles("w1_bf1", [P, 2 * P, 4], BF16, 2),
         ]
-        x_codes = [keep.tile([P, S], U32, name="x_codes%d" % s, align_bytes=64) for s in range(2)]
-        x_scales = [keep.tile([P, S], U8, name="x_scales%d" % s, align_bytes=64) for s in range(2)]
-        w1_bf = [keep.tile([P, 4 * H], BF16, name="w1_bf%d" % s, align_bytes=64) for s in range(2)]
-        w1_codes = [keep.tile([P, H], U32, name="w1_codes%d" % s, align_bytes=64) for s in range(2)]
-        w1_scales = [keep.tile([P, H], U8, name="w1_scales%d" % s, align_bytes=64) for s in range(2)]
-        w2_codes = keep.tile([P, N], U32, name="w2_codes", align_bytes=64)
-        w2_scales = keep.tile([P, N], U8, name="w2_scales", align_bytes=64)
-        r = [keep.tile([P, 4, n], F32, name="r%d" % n) for n in (CH, S - CH)]
-        h_bf = [keep.tile([P, CH, 4], BF16, name="h_bf%d" % c, align_bytes=64) for c in range(CHUNKS)]
-        h_codes = [keep.tile([P, CH], U32, name="h_codes%d" % c, align_bytes=64) for c in range(CHUNKS)]
-        h_scales = [keep.tile([P, CH], U8, name="h_scales%d" % c, align_bytes=64) for c in range(CHUNKS)]
-        y = [[keep.tile([P, 2, CH], F32, name="y%d%d" % (c, b)) for b in range(2)] for c in range(CHUNKS)]
+        w1_codes = tiles("w1_codes", [P, 2 * P], U32, 2, 2)
+        w1_scales = tiles("w1_scales", [P, 2 * P], U8, 2, 2)
+        w2_bf = tiles("w2_bf", [P, N // 2, 4], BF16, 2)
+        w2_codes = tiles("w2_codes", [P, N // 2], U32, 2)
+        w2_scales = tiles("w2_scales", [P, N // 2], U8, 2)
+        r = tiles("r", [P, 4, CH], F32, CHUNKS)
+        h_bf = tiles("h_bf", [P, CH, 4], BF16, CHUNKS)
+        h_codes = tiles("h_codes", [P, CH], U32, CHUNKS)
+        h_scales = tiles("h_scales", [P, CH], U8, CHUNKS)
+        y = tiles("y", [P, 2, CH], F32, CHUNKS, 2)
 
         def chunk(c):
             return slice(CH * c, CH * (c + 1))
@@ -86,82 +85,72 @@ def tile_picked_pick_mlp_relu2_srt_e_kernel(tc, xT, w1, w2, offs, out):
             )
 
         def quantize(codes, scales, values):
-            nc.vector.quantize_mx(out=codes.bitcast(FP8X4), scales=scales, in_=values)
+            nc.vector.quantize_mx(out=codes.bitcast(FP8X4), scales=scales, in_=values.rearrange("p n t -> p (n t)"))
 
-        def gather(s, j):
-            nc.vector.tensor_copy(picked[s][:, j, :], x[s][j][:].indirect(offsets[:]))
-
-        def gather_part(first, last, width):
+        def gather(s, j, first=0, last=S):
+            width = T - S + last
             nc.vector.tensor_copy(
-                picked[1][:, 3, first:last],
-                x[1][3][:, 0:width].indirect(offsets[:, first // 16 : last // 16]),
+                picked[s][:, j, first:last],
+                x[s][j][:, 0:width].indirect(offsets[:, first // 16 : last // 16]),
             )
 
         def x_interleave(copy, s, c):
-            interleave(copy, x_bf[s][:, chunk(c), :], picked[s][:, :, chunk(c)])
+            interleave(copy, x_bf[s][c][:], picked[s][:, :, chunk(c)])
 
         def x_quantize(s, c):
-            quantize(
-                x_codes[s][:, chunk(c)],
-                x_scales[s][:, chunk(c)],
-                x_bf[s][:, chunk(c), :].rearrange("p n t -> p (n t)"),
-            )
+            g = min(c, 1)
+            cols = chunk(c - g)
+            quantize(x_codes[g][s][:, cols], x_scales[g][s][:, cols], x_bf[s][c][:])
 
-        def w1_interleave(copy, s, half):
-            tiles = slice(2 * half, 2 * half + 2)
+        def w1_interleave(copy, s, u):
             copy(
-                out=w1_bf[s][:].rearrange("p (t m j) -> p m t j", t=4, j=4)[:, :, tiles, :],
-                in_=w1_raw[s][:].rearrange("p j (m t) -> p m t j", t=4)[:, :, tiles, :],
+                out=w1_bf[s][u][:].rearrange("p (t m) j -> p m t j", t=2),
+                in_=w1_raw[s][:].rearrange("p j (m t) -> p m t j", t=4)[:, :, 2 * u : 2 * u + 2, :],
             )
 
-        def w1_quantize(s):
-            quantize(w1_codes[s][:], w1_scales[s][:], w1_bf[s][:])
+        def w1_quantize(s, u):
+            quantize(w1_codes[s][u][:], w1_scales[s][u][:], w1_bf[s][u][:])
 
-        w2_bf_tile = []
+        def w2_interleave(copy, b, half):
+            n = slice(P * half, P * (half + 1))
+            interleave(copy, w2_bf[b][:, n, :], w2_raw[b][:, :, n])
 
-        def w2_interleave(copy, q):
-            w2_bf = w2_bf_tile[0]
-            n = slice(P * q, P * (q + 1))
-            interleave(copy, w2_bf[:, n, :], w2_raw[:, :, n])
-
-        def w2_quantize(half):
-            w2_bf = w2_bf_tile[0]
-            n = slice(N // 2 * half, N // 2 * (half + 1))
-            quantize(w2_codes[:, n], w2_scales[:, n], w2_bf[:, n, :].rearrange("p n t -> p (n t)"))
+        def w2_quantize(b):
+            quantize(w2_codes[b][:], w2_scales[b][:], w2_bf[b][:])
 
         group_cols = [slice(0, CH), slice(CH, S)]
-        banks = [[], []]
+        banks = {}
 
         def mm1(g, s, t):
             cols = group_cols[g]
             width = cols.stop - cols.start
             if s == 0:
-                bank = psum.tile([P, 512], F32, name="bank")
-                banks[g].append(bank)
-            block = slice(P * t, P * (t + 1))
+                banks[g, t] = psum.tile([P, 512], F32, name="bank")
+            block = slice(P * (t % 2), P * (t % 2 + 1))
             nc.tensor.matmul_mx(
-                out=banks[g][t][:, 0:width],
-                lhsT=w1_codes[s][:, block].bitcast(FP8X4),
-                lhsT_scale=w1_scales[s][:, block],
-                rhs=x_codes[s][:, cols].bitcast(FP8X4),
-                rhs_scale=x_scales[s][:, cols],
+                out=banks[g, t][:, 0:width],
+                lhsT=w1_codes[s][t // 2][:, block].bitcast(FP8X4),
+                lhsT_scale=w1_scales[s][t // 2][:, block],
+                rhs=x_codes[g][s][:].bitcast(FP8X4),
+                rhs_scale=x_scales[g][s][:],
                 start=(s == 0),
                 stop=(s == 1),
             )
 
-        def relu_scalar(g, t):
-            width = r[g].shape[2]
-            nc.scalar.activation(r[g][:, t, :], banks[g][t][:, 0:width], RELU)
+        def bank_cols(c, t):
+            g = min(c, 1)
+            first = CH * c - group_cols[g].start
+            return banks[g, t][:, first : first + CH]
 
-        def relu_vector(g, t):
-            width = r[g].shape[2]
-            nc.vector.tensor_scalar_max(r[g][:, t, :], banks[g][t][:, 0:width], 0.0)
+        def relu_scalar(c, t):
+            nc.scalar.activation(r[c][:, t, :], bank_cols(c, t), RELU)
+
+        def relu_vector(c, t):
+            nc.vector.tensor_scalar_max(r[c][:, t, :], bank_cols(c, t), 0.0)
 
         def square_views(c, half):
-            g = 0 if c == 0 else 1
-            first = CH * c - group_cols[g].start + CH // 2 * half
-            src = r[g][:, :, first : first + CH // 2].rearrange("p t (c i) -> p c t i", i=4)
             n = slice(CH // 2 * half, CH // 2 * (half + 1))
+            src = r[c][:, :, n].rearrange("p t (c i) -> p c t i", i=4)
             return h_bf[c][:, n, :].rearrange("p (c i) t -> p c t i", i=4), src
 
         def square_scalar(c, half):
@@ -173,18 +162,18 @@ def tile_picked_pick_mlp_relu2_srt_e_kernel(tc, xT, w1, w2, offs, out):
             nc.vector.tensor_tensor(dst, src, src, MULT)
 
         def h_quantize(c):
-            quantize(h_codes[c][:], h_scales[c][:], h_bf[c][:].rearrange("p n t -> p (n t)"))
+            quantize(h_codes[c][:], h_scales[c][:], h_bf[c][:])
 
         y_banks = {}
 
         def mm2(c, b):
             bank = psum.tile([P, 512], F32, name="bank")
             for i in range(2):
-                block = slice(P * (2 * b + i), P * (2 * b + i + 1))
+                block = slice(P * i, P * (i + 1))
                 nc.tensor.matmul_mx(
                     out=bank[:, CH * i : CH * (i + 1)],
-                    lhsT=w2_codes[:, block].bitcast(FP8X4),
-                    lhsT_scale=w2_scales[:, block],
+                    lhsT=w2_codes[b][:, block].bitcast(FP8X4),
+                    lhsT_scale=w2_scales[b][:, block],
                     rhs=h_codes[c][:].bitcast(FP8X4),
                     rhs_scale=h_scales[c][:],
                     start=True,
@@ -196,78 +185,111 @@ def tile_picked_pick_mlp_relu2_srt_e_kernel(tc, xT, w1, w2, offs, out):
             copy(out=y[c][b][:].rearrange("p i n -> p (i n)"), in_=y_banks[c, b][:])
             nc.sync.dma_start(out_view[b][:, :, chunk(c)], y[c][b][:])
 
+        def mm2_block(c, q):
+            bank = psum.tile([P, 512], F32, name="bank")
+            block = slice(P * (q % 2), P * (q % 2 + 1))
+            nc.tensor.matmul_mx(
+                out=bank[:, 0:CH],
+                lhsT=w2_codes[q // 2][:, block].bitcast(FP8X4),
+                lhsT_scale=w2_scales[q // 2][:, block],
+                rhs=h_codes[c][:].bitcast(FP8X4),
+                rhs_scale=h_scales[c][:],
+                start=True,
+                stop=True,
+            )
+            y_banks[c, 2 + q] = bank
+
+        def store_block(copy, c, q):
+            copy(out=y[c][q // 2][:, q % 2, :], in_=y_banks[c, 2 + q][:, 0:CH])
+            nc.sync.dma_start(out_view[q // 2][:, q % 2, chunk(c)], y[c][q // 2][:, q % 2, :])
+
         on_scalar = nc.scalar.copy
         on_vector = nc.vector.tensor_copy
 
-        gather(0, 0)
-        w1_interleave(on_scalar, 0, 0)
-        w1_interleave(on_scalar, 0, 1)
-        gather(0, 1)
-        w1_quantize(0)
-        gather(0, 2)
-        gather(0, 3)
-        x_interleave(on_scalar, 0, 0)
-        x_interleave(on_vector, 0, 1)
-        x_interleave(on_scalar, 0, 2)
+        for j in range(3):
+            gather(0, j)
+        for c in range(CHUNKS):
+            gather(0, 3, CH * c, CH * (c + 1))
+            x_interleave(on_scalar, 0, c)
         gather(1, 0)
-        x_quantize(0, 0)
-        x_quantize(0, 1)
-        w1_interleave(on_scalar, 1, 0)
-        w1_interleave(on_scalar, 1, 1)
+        for c in range(CHUNKS):
+            x_quantize(0, c)
         gather(1, 1)
-        for t in range(4):
-            mm1(0, 0, t)
-        x_quantize(0, 2)
-        for t in range(4):
-            mm1(1, 0, t)
-        w1_quantize(1)
         gather(1, 2)
-
-        gather_part(0, CH, HEAD)
-        gather_part(CH, S, T)
+        for c in range(CHUNKS):
+            gather(1, 3, CH * c, CH * (c + 1))
         x_interleave(on_scalar, 1, 0)
         x_interleave(on_scalar, 1, 1)
         x_interleave(on_vector, 1, 2)
-        for c in range(CHUNKS):
-            x_quantize(1, c)
+        x_quantize(1, 0)
+        warm = psum.tile([P, 512], F32, name="bank")
+        for turn in range(2):
+            nc.tensor.matmul_mx(
+                out=warm[:],
+                lhsT=x_codes[0][1][:, 0:P].bitcast(FP8X4),
+                lhsT_scale=x_scales[0][1][:, 0:P],
+                rhs=x_codes[1][0][:].bitcast(FP8X4),
+                rhs_scale=x_scales[1][0][:],
+                start=True,
+                stop=True,
+            )
+        w1_interleave(on_vector, 0, 0)
+        w1_interleave(on_scalar, 0, 1)
+        w1_quantize(0, 0)
+        x_codes[1].append(keep.tile([P, S - CH], U32, name="x_codes_late", tag="shared", align_bytes=64))
+        x_quantize(1, 2)
+        w1_quantize(0, 1)
+        for t in range(4):
+            mm1(0, 0, t)
+        w1_interleave(on_vector, 1, 0)
+        w1_interleave(on_scalar, 1, 1)
+        x_quantize(1, 1)
+        w1_quantize(1, 0)
+        w1_quantize(1, 1)
         for t in range(4):
             mm1(0, 1, t)
-        relu_scalar(0, 0)
-        relu_vector(0, 1)
-        relu_scalar(0, 2)
-        relu_scalar(0, 3)
-        for t in range(4):
-            mm1(1, 1, t)
-        w2_bf = turns.tile([P, N, 4], BF16, name="w2_bf", tag="bf", align_bytes=64)
-        w2_bf_tile.append(w2_bf)
-        w2_interleave(on_vector, 2)
-        w2_interleave(on_vector, 1)
-        w2_interleave(on_scalar, 0)
+        for s in range(2):
+            for t in range(4):
+                mm1(1, s, t)
+
+        def relu(c, on_vector_count):
+            for t in range(4):
+                if t < on_vector_count:
+                    relu_vector(c, t)
+                else:
+                    relu_scalar(c, t)
+
+        def product(c):
+            mm2(c, 0)
+            mm2(c, 1)
+
+        w2_interleave(on_scalar, 0, 0)
+        w2_interleave(on_scalar, 0, 1)
+        relu(0, 2)
         w2_quantize(0)
-        relu_scalar(1, 0)
-        square_scalar(0, 0)
-        square_vector(0, 1)
-        relu_vector(1, 1)
-        relu_scalar(1, 2)
-        relu_vector(1, 3)
+        square_vector(0, 0)
+        square_scalar(0, 1)
+        relu(1, 1)
         h_quantize(0)
-        w2_interleave(on_scalar, 3)
-        w2_quantize(1)
-        square_vector(1, 0)
+        w2_interleave(on_vector, 1, 0)
+        w2_interleave(on_vector, 1, 1)
         square_scalar(1, 1)
+        square_vector(1, 0)
+        w2_quantize(1)
+        product(0)
+        relu(2, 0)
         h_quantize(1)
-        square_vector(2, 0)
+        product(1)
+        store(on_vector, 0, 0)
         square_scalar(2, 1)
-        mm2(0, 0)
-        mm2(0, 1)
-        store(on_scalar, 0, 0)
+        square_vector(2, 0)
         store(on_scalar, 0, 1)
-        mm2(1, 0)
-        mm2(1, 1)
         h_quantize(2)
+
+        for q in range(4):
+            mm2_block(2, q)
         store(on_vector, 1, 0)
         store(on_scalar, 1, 1)
-        mm2(2, 0)
-        mm2(2, 1)
-        store(on_scalar, 2, 0)
-        store(on_vector, 2, 1)
+
+        for q in range(4):
+            store_block((on_scalar, on_vector)[q % 2], 2, q)

@@ -121,10 +121,10 @@ def tile_picked_pick_mlp_relu2_srt_e_kernel(tc, xT, w1, w2, offs, out):
         group_cols = [slice(0, CH), slice(CH, S)]
         banks = {}
 
-        def mm1(g, s, t):
+        def mm1(g, s, t, first=0):
             cols = group_cols[g]
             width = cols.stop - cols.start
-            if s == 0:
+            if s == first:
                 banks[g, t] = psum.tile([P, 512], F32, name="bank")
             block = slice(P * (t % 2), P * (t % 2 + 1))
             nc.tensor.matmul_mx(
@@ -133,8 +133,8 @@ def tile_picked_pick_mlp_relu2_srt_e_kernel(tc, xT, w1, w2, offs, out):
                 lhsT_scale=w1_scales[s][t // 2][:, block],
                 rhs=x_codes[g][s][:].bitcast(FP8X4),
                 rhs_scale=x_scales[g][s][:],
-                start=(s == 0),
-                stop=(s == 1),
+                start=(s == first),
+                stop=(s != first),
             )
 
         def bank_cols(c, t):
@@ -222,17 +222,6 @@ def tile_picked_pick_mlp_relu2_srt_e_kernel(tc, xT, w1, w2, offs, out):
         x_interleave(on_scalar, 1, 1)
         x_interleave(on_vector, 1, 2)
         x_quantize(1, 0)
-        warm = psum.tile([P, 512], F32, name="bank")
-        for turn in range(2):
-            nc.tensor.matmul_mx(
-                out=warm[:],
-                lhsT=x_codes[0][1][:, 0:P].bitcast(FP8X4),
-                lhsT_scale=x_scales[0][1][:, 0:P],
-                rhs=x_codes[1][0][:].bitcast(FP8X4),
-                rhs_scale=x_scales[1][0][:],
-                start=True,
-                stop=True,
-            )
         w1_interleave(on_vector, 0, 0)
         w1_interleave(on_scalar, 0, 1)
         w1_quantize(0, 0)
@@ -249,8 +238,11 @@ def tile_picked_pick_mlp_relu2_srt_e_kernel(tc, xT, w1, w2, offs, out):
         for t in range(4):
             mm1(0, 1, t)
         for s in range(2):
-            for t in range(4):
+            for t in range(2):
                 mm1(1, s, t)
+        for t in range(2, 4):
+            mm1(1, 1, t, first=1)
+            mm1(1, 0, t, first=1)
 
         def relu(c, on_vector_count):
             for t in range(4):

@@ -16,9 +16,14 @@ SQUARE = mybir.ActivationFunctionType.Square
 MULT = mybir.AluOpType.mult
 
 P = 128
+SLOTS = 4
+PASSES = K // (P * SLOTS)
 CH = 256
 CHUNKS = S // CH
 HEAD = T - S + CH
+BANK = 512
+PER_COLUMN = 16
+ALIGN = 64
 
 
 def tile_picked_pick_mlp_relu2_srt_e_kernel(tc, xT, w1, w2, offs, out):
@@ -27,75 +32,91 @@ def tile_picked_pick_mlp_relu2_srt_e_kernel(tc, xT, w1, w2, offs, out):
         keep = ctx.enter_context(tc.tile_pool(name="keep", bufs=1))
         psum = ctx.enter_context(tc.psum_pool(name="psum", bufs=8))
 
-        x_view = xT.rearrange("(s p j) t -> s j p t", s=2, j=4)
-        w1_view = w1.rearrange("(s p j) c -> s p j c", s=2, j=4)
-        w2_view = w2.rearrange("(p j) (b c) -> b p j c", j=4, b=2)
+        x_view = xT.rearrange("(s p j) t -> s j p t", s=PASSES, j=SLOTS)
+        w1_view = w1.rearrange("(s p j) c -> s p j c", s=PASSES, j=SLOTS)
+        w2_view = w2.rearrange("(p j) (b c) -> b p j c", j=SLOTS, b=2)
         out_view = out.rearrange("(b i p) n -> b p i n", b=2, i=2)
 
-        offsets = keep.tile([P, S // 16], U16, name="offsets")
-        x = [[keep.tile([P, T], F32, name="x%d%d" % (s, j)) for j in range(4)] for s in range(2)]
-        w1_raw = [keep.tile([P, 4, H], F32, name="w1_raw%d" % s) for s in range(2)]
-        w2_raw = [keep.tile([P, 4, N // 2], F32, name="w2_raw%d" % b) for b in range(2)]
+        offsets = keep.tile([P, S // PER_COLUMN], U16, name="offsets")
+        x = [[keep.tile([P, T], F32, name="x%d%d" % (s, j)) for j in range(SLOTS)] for s in range(PASSES)]
+        w1_raw = [keep.tile([P, SLOTS, H], F32, name="w1_raw%d" % s) for s in range(PASSES)]
+        w2_raw = [keep.tile([P, SLOTS, N // 2], F32, name="w2_raw%d" % b) for b in range(2)]
 
+        planes = [(s, j) for s in range(PASSES) for j in range(SLOTS)]
         nc.sync.dma_start(x[0][0][:], x_view[0, 0])
         nc.sync.dma_start(offsets[:], offs)
-        for s, j in [(0, 1), (0, 2), (0, 3), (1, 0), (1, 1), (1, 2)]:
+        for s, j in planes[1:-1]:
             nc.sync.dma_start(x[s][j][:], x_view[s, j])
         for cols in (slice(0, HEAD), slice(HEAD, T)):
             nc.sync.dma_start(x[1][3][:, cols], x_view[1, 3][:, cols])
-        for s in range(2):
+        for s in range(PASSES):
             nc.sync.dma_start(w1_raw[s][:], w1_view[s])
         for b in range(2):
             nc.sync.dma_start(w2_raw[b][:], w2_view[b])
 
         def tiles(name, shape, dtype, *counts):
             if len(counts) == 1:
-                return [keep.tile(shape, dtype, name="%s_%d" % (name, a), align_bytes=64) for a in range(counts[0])]
+                return [keep.tile(shape, dtype, name="%s_%d" % (name, a), align_bytes=ALIGN) for a in range(counts[0])]
             return [tiles("%s_%d" % (name, a), shape, dtype, *counts[1:]) for a in range(counts[0])]
 
-        picked = tiles("picked", [P, 4, S], F32, 2)
-        x_bf = tiles("x_bf", [P, CH, 4], BF16, 2, CHUNKS)
-        x_codes = [tiles("x_codes_first", [P, CH], U32, 2), tiles("x_codes_rest", [P, S - CH], U32, 1)]
-        x_scales = [tiles("x_scales_first", [P, CH], U8, 2), tiles("x_scales_rest", [P, S - CH], U8, 2)]
+        picked = tiles("picked", [P, SLOTS, S], F32, PASSES)
+        x_bf = tiles("x_bf", [P, CH, SLOTS], BF16, PASSES, CHUNKS)
+        x_codes = [tiles("x_codes_first", [P, CH], U32, PASSES), tiles("x_codes_rest", [P, S - CH], U32, 1)]
+        x_scales = [tiles("x_scales_first", [P, CH], U8, PASSES), tiles("x_scales_rest", [P, S - CH], U8, PASSES)]
         w1_bf = [
             [
-                keep.tile([P, 2 * P, 4], BF16, name="w1_bf00", tag="shared", align_bytes=64),
-                keep.tile([P, 2 * P, 4], BF16, name="w1_bf01", align_bytes=64),
+                keep.tile([P, 2 * P, SLOTS], BF16, name="w1_bf00", tag="shared", align_bytes=ALIGN),
+                keep.tile([P, 2 * P, SLOTS], BF16, name="w1_bf01", align_bytes=ALIGN),
             ],
-            tiles("w1_bf1", [P, 2 * P, 4], BF16, 2),
+            tiles("w1_bf1", [P, 2 * P, SLOTS], BF16, 2),
         ]
-        w1_codes = tiles("w1_codes", [P, 2 * P], U32, 2, 2)
-        w1_scales = tiles("w1_scales", [P, 2 * P], U8, 2, 2)
-        w2_bf = tiles("w2_bf", [P, N // 2, 4], BF16, 2)
+        w1_codes = tiles("w1_codes", [P, 2 * P], U32, PASSES, 2)
+        w1_scales = tiles("w1_scales", [P, 2 * P], U8, PASSES, 2)
+        w2_bf = tiles("w2_bf", [P, N // 2, SLOTS], BF16, 2)
         w2_codes = tiles("w2_codes", [P, N // 2], U32, 2)
         w2_scales = tiles("w2_scales", [P, N // 2], U8, 2)
-        r = tiles("r", [P, 4, CH], F32, CHUNKS)
-        h_bf = tiles("h_bf", [P, CH, 4], BF16, CHUNKS)
+        r = tiles("r", [P, SLOTS, CH], F32, CHUNKS)
+        h_bf = tiles("h_bf", [P, CH, SLOTS], BF16, CHUNKS)
         h_codes = tiles("h_codes", [P, CH], U32, CHUNKS)
         h_scales = tiles("h_scales", [P, CH], U8, CHUNKS)
         y = tiles("y", [P, 2, CH], F32, CHUNKS, 2)
 
+        on_scalar = nc.scalar.copy
+        on_vector = nc.vector.tensor_copy
+
         def chunk(c):
             return slice(CH * c, CH * (c + 1))
 
+        def slot_views(dst, src):
+            return dst.rearrange("p (c i) t -> p c t i", i=4), src.rearrange("p t (c i) -> p c t i", i=4)
+
         def interleave(copy, dst, src):
-            copy(
-                out=dst.rearrange("p (c i) t -> p c t i", i=4),
-                in_=src.rearrange("p t (c i) -> p c t i", i=4),
-            )
+            dst_view, src_view = slot_views(dst, src)
+            copy(out=dst_view, in_=src_view)
 
         def quantize(codes, scales, values):
             nc.vector.quantize_mx(out=codes.bitcast(FP8X4), scales=scales, in_=values.rearrange("p n t -> p (n t)"))
 
-        def gather(s, j, first=0, last=S):
-            width = T - S + last
-            nc.vector.tensor_copy(
-                picked[s][:, j, first:last],
-                x[s][j][:, 0:width].indirect(offsets[:, first // 16 : last // 16]),
+        def matmul(dst, w_codes, w_scales, codes, scales, start, stop):
+            nc.tensor.matmul_mx(
+                out=dst,
+                lhsT=w_codes.bitcast(FP8X4),
+                lhsT_scale=w_scales,
+                rhs=codes.bitcast(FP8X4),
+                rhs_scale=scales,
+                start=start,
+                stop=stop,
             )
 
-        def x_interleave(copy, s, c):
-            interleave(copy, x_bf[s][c][:], picked[s][:, :, chunk(c)])
+        def gather(s, j, first=0, last=S):
+            window = x[s][j][:, 0 : T - S + last]
+            entries = offsets[:, first // PER_COLUMN : last // PER_COLUMN]
+            nc.vector.tensor_copy(picked[s][:, j, first:last], window.indirect(entries))
+
+        def finish_pass(s):
+            for c in range(CHUNKS):
+                gather(s, SLOTS - 1, CH * c, CH * (c + 1))
+                interleave(on_scalar, x_bf[s][c][:], picked[s][:, :, chunk(c)])
 
         def x_quantize(s, c):
             g = min(c, 1)
@@ -104,184 +125,144 @@ def tile_picked_pick_mlp_relu2_srt_e_kernel(tc, xT, w1, w2, offs, out):
 
         def w1_interleave(copy, s, u):
             copy(
-                out=w1_bf[s][u][:].rearrange("p (t m) j -> p m t j", t=2),
-                in_=w1_raw[s][:].rearrange("p j (m t) -> p m t j", t=4)[:, :, 2 * u : 2 * u + 2, :],
+                out=w1_bf[s][u][:].rearrange("p (t m) j -> p m j t", t=2),
+                in_=w1_raw[s][:].rearrange("p j (m t) -> p m j t", t=SLOTS)[:, :, :, 2 * u : 2 * u + 2],
             )
 
         def w1_quantize(s, u):
             quantize(w1_codes[s][u][:], w1_scales[s][u][:], w1_bf[s][u][:])
 
-        def w2_interleave(copy, b, half):
-            n = slice(P * half, P * (half + 1))
+        def w2_interleave(copy, b, i):
+            n = slice(P * i, P * (i + 1))
             interleave(copy, w2_bf[b][:, n, :], w2_raw[b][:, :, n])
 
         def w2_quantize(b):
             quantize(w2_codes[b][:], w2_scales[b][:], w2_bf[b][:])
 
-        group_cols = [slice(0, CH), slice(CH, S)]
-        banks = {}
+        v_banks = {}
 
-        def mm1(g, s, t, first=0):
-            cols = group_cols[g]
-            width = cols.stop - cols.start
-            if s == first:
-                banks[g, t] = psum.tile([P, 512], F32, name="bank")
+        def first_product(g, s, t, opening=0):
+            if s == opening:
+                v_banks[g, t] = psum.tile([P, BANK], F32, name="bank")
             block = slice(P * (t % 2), P * (t % 2 + 1))
-            nc.tensor.matmul_mx(
-                out=banks[g, t][:, 0:width],
-                lhsT=w1_codes[s][t // 2][:, block].bitcast(FP8X4),
-                lhsT_scale=w1_scales[s][t // 2][:, block],
-                rhs=x_codes[g][s][:].bitcast(FP8X4),
-                rhs_scale=x_scales[g][s][:],
-                start=(s == first),
-                stop=(s != first),
+            matmul(
+                v_banks[g, t][:, 0 : x_codes[g][s].shape[1]],
+                w1_codes[s][t // 2][:, block],
+                w1_scales[s][t // 2][:, block],
+                x_codes[g][s][:],
+                x_scales[g][s][:],
+                start=(s == opening),
+                stop=(s != opening),
             )
 
-        def bank_cols(c, t):
+        def relu(c, vector_blocks):
             g = min(c, 1)
-            first = CH * c - group_cols[g].start
-            return banks[g, t][:, first : first + CH]
-
-        def relu_scalar(c, t):
-            nc.scalar.activation(r[c][:, t, :], bank_cols(c, t), RELU)
-
-        def relu_vector(c, t):
-            nc.vector.tensor_scalar_max(r[c][:, t, :], bank_cols(c, t), 0.0)
+            for t in range(SLOTS):
+                v = v_banks[g, t][:, chunk(c - g)]
+                if t < vector_blocks:
+                    nc.vector.tensor_scalar_max(r[c][:, t, :], v, 0.0)
+                else:
+                    nc.scalar.activation(r[c][:, t, :], v, RELU)
 
         def square_views(c, half):
             n = slice(CH // 2 * half, CH // 2 * (half + 1))
-            src = r[c][:, :, n].rearrange("p t (c i) -> p c t i", i=4)
-            return h_bf[c][:, n, :].rearrange("p (c i) t -> p c t i", i=4), src
+            return slot_views(h_bf[c][:, n, :], r[c][:, :, n])
 
-        def square_scalar(c, half):
-            dst, src = square_views(c, half)
-            nc.scalar.activation(dst, src, SQUARE)
-
-        def square_vector(c, half):
-            dst, src = square_views(c, half)
+        def square_vector(c):
+            dst, src = square_views(c, 0)
             nc.vector.tensor_tensor(dst, src, src, MULT)
+
+        def square_scalar(c):
+            dst, src = square_views(c, 1)
+            nc.scalar.activation(dst, src, SQUARE)
 
         def h_quantize(c):
             quantize(h_codes[c][:], h_scales[c][:], h_bf[c][:])
 
-        y_banks = {}
+        def second_product(dst, c, b, i):
+            block = slice(P * i, P * (i + 1))
+            matmul(dst, w2_codes[b][:, block], w2_scales[b][:, block], h_codes[c][:], h_scales[c][:], True, True)
 
-        def mm2(c, b):
-            bank = psum.tile([P, 512], F32, name="bank")
-            for i in range(2):
-                block = slice(P * i, P * (i + 1))
-                nc.tensor.matmul_mx(
-                    out=bank[:, CH * i : CH * (i + 1)],
-                    lhsT=w2_codes[b][:, block].bitcast(FP8X4),
-                    lhsT_scale=w2_scales[b][:, block],
-                    rhs=h_codes[c][:].bitcast(FP8X4),
-                    rhs_scale=h_scales[c][:],
-                    start=True,
-                    stop=True,
-                )
-            y_banks[c, b] = bank
+        def product_by_halves(c):
+            banks = []
+            for b in range(2):
+                bank = psum.tile([P, BANK], F32, name="bank")
+                for i in range(2):
+                    second_product(bank[:, chunk(i)], c, b, i)
+                banks.append(bank)
+            return banks
 
-        def store(copy, c, b):
-            copy(out=y[c][b][:].rearrange("p i n -> p (i n)"), in_=y_banks[c, b][:])
+        def product_by_blocks(c):
+            banks = []
+            for b in range(2):
+                for i in range(2):
+                    bank = psum.tile([P, BANK], F32, name="bank")
+                    second_product(bank[:, 0:CH], c, b, i)
+                    banks.append(bank)
+            return banks
+
+        def store_half(copy, bank, c, b):
+            copy(out=y[c][b][:].rearrange("p i n -> p (i n)"), in_=bank[:])
             nc.sync.dma_start(out_view[b][:, :, chunk(c)], y[c][b][:])
 
-        def mm2_block(c, q):
-            bank = psum.tile([P, 512], F32, name="bank")
-            block = slice(P * (q % 2), P * (q % 2 + 1))
-            nc.tensor.matmul_mx(
-                out=bank[:, 0:CH],
-                lhsT=w2_codes[q // 2][:, block].bitcast(FP8X4),
-                lhsT_scale=w2_scales[q // 2][:, block],
-                rhs=h_codes[c][:].bitcast(FP8X4),
-                rhs_scale=h_scales[c][:],
-                start=True,
-                stop=True,
-            )
-            y_banks[c, 2 + q] = bank
-
-        def store_block(copy, c, q):
-            copy(out=y[c][q // 2][:, q % 2, :], in_=y_banks[c, 2 + q][:, 0:CH])
-            nc.sync.dma_start(out_view[q // 2][:, q % 2, chunk(c)], y[c][q // 2][:, q % 2, :])
-
-        on_scalar = nc.scalar.copy
-        on_vector = nc.vector.tensor_copy
-
-        for j in range(3):
+        for j in range(SLOTS - 1):
             gather(0, j)
-        for c in range(CHUNKS):
-            gather(0, 3, CH * c, CH * (c + 1))
-            x_interleave(on_scalar, 0, c)
+        finish_pass(0)
         gather(1, 0)
         for c in range(CHUNKS):
             x_quantize(0, c)
         gather(1, 1)
         gather(1, 2)
-        for c in range(CHUNKS):
-            gather(1, 3, CH * c, CH * (c + 1))
-        x_interleave(on_scalar, 1, 0)
-        x_interleave(on_scalar, 1, 1)
-        x_interleave(on_vector, 1, 2)
+        finish_pass(1)
         x_quantize(1, 0)
-        w1_interleave(on_vector, 0, 0)
-        w1_interleave(on_scalar, 0, 1)
-        w1_quantize(0, 0)
-        x_codes[1].append(keep.tile([P, S - CH], U32, name="x_codes_late", tag="shared", align_bytes=64))
-        x_quantize(1, 2)
-        w1_quantize(0, 1)
-        for t in range(4):
-            mm1(0, 0, t)
+
+        for u in range(2):
+            w1_interleave(on_vector, 0, u)
+        for u in range(2):
+            w1_quantize(0, u)
+        x_codes[1].append(keep.tile([P, S - CH], U32, name="x_codes_late", tag="shared", align_bytes=ALIGN))
+        x_quantize(1, 1)
+        for t in range(SLOTS):
+            first_product(0, 0, t)
+
         w1_interleave(on_vector, 1, 0)
         w1_interleave(on_scalar, 1, 1)
-        x_quantize(1, 1)
-        w1_quantize(1, 0)
-        w1_quantize(1, 1)
-        for t in range(4):
-            mm1(0, 1, t)
-        for s in range(2):
-            for t in range(2):
-                mm1(1, s, t)
-        for t in range(2, 4):
-            mm1(1, 1, t, first=1)
-            mm1(1, 0, t, first=1)
+        x_quantize(1, 2)
+        for u in range(2):
+            w1_quantize(1, u)
+        for t in range(SLOTS):
+            first_product(0, 1, t)
+        for t in range(SLOTS):
+            opening = t // 2
+            first_product(1, opening, t, opening)
+            first_product(1, 1 - opening, t, opening)
 
-        def relu(c, on_vector_count):
-            for t in range(4):
-                if t < on_vector_count:
-                    relu_vector(c, t)
-                else:
-                    relu_scalar(c, t)
-
-        def product(c):
-            mm2(c, 0)
-            mm2(c, 1)
-
-        w2_interleave(on_scalar, 0, 0)
-        w2_interleave(on_scalar, 0, 1)
+        for i in range(2):
+            w2_interleave(on_scalar, 0, i)
         relu(0, 2)
         w2_quantize(0)
-        square_vector(0, 0)
-        square_scalar(0, 1)
+        square_vector(0)
+        square_scalar(0)
         relu(1, 1)
         h_quantize(0)
-        w2_interleave(on_vector, 1, 0)
-        w2_interleave(on_vector, 1, 1)
-        square_scalar(1, 1)
-        square_vector(1, 0)
+        for i in range(2):
+            w2_interleave(on_vector, 1, i)
+        square_scalar(1)
+        square_vector(1)
         w2_quantize(1)
-        product(0)
+        banks_0 = product_by_halves(0)
         relu(2, 0)
         h_quantize(1)
-        product(1)
-        store(on_vector, 0, 0)
-        square_scalar(2, 1)
-        square_vector(2, 0)
-        store(on_scalar, 0, 1)
+        banks_1 = product_by_halves(1)
+        store_half(on_vector, banks_0[0], 0, 0)
+        square_scalar(2)
+        square_vector(2)
+        store_half(on_scalar, banks_0[1], 0, 1)
         h_quantize(2)
-
-        for q in range(4):
-            mm2_block(2, q)
-        store(on_vector, 1, 0)
-        store(on_scalar, 1, 1)
-
-        for q in range(4):
-            store_block((on_scalar, on_vector)[q % 2], 2, q)
+        banks_2 = product_by_blocks(2)
+        store_half(on_vector, banks_1[0], 1, 0)
+        store_half(on_scalar, banks_1[1], 1, 1)
+        for b in range(2):
+            for i in range(2):
+                (on_scalar, on_vector)[i](out=y[2][b][:, i, :], in_=banks_2[2 * b + i][:, 0:CH])
+                nc.sync.dma_start(out_view[b][:, i, chunk(2)], y[2][b][:, i, :])

@@ -23,6 +23,7 @@ CHUNKS = S // CH
 HEAD = T - S + CH
 BANK = 512
 PER_COLUMN = 16
+SHARE = 88
 ALIGN = 64
 
 
@@ -123,10 +124,10 @@ def tile_picked_pick_mlp_relu2_srt_e_kernel(tc, xT, w1, w2, offs, out):
             cols = chunk(c - g)
             quantize(x_codes[g][s][:, cols], x_scales[g][s][:, cols], x_bf[s][c][:])
 
-        def w1_interleave(copy, s, u):
+        def w1_interleave(copy, s, u, first=0, last=P):
             copy(
-                out=w1_bf[s][u][:].rearrange("p (t m) j -> p m j t", t=2),
-                in_=w1_raw[s][:].rearrange("p j (m t) -> p m j t", t=SLOTS)[:, :, :, 2 * u : 2 * u + 2],
+                out=w1_bf[s][u][:].rearrange("p (t m) j -> p m j t", t=2)[:, first:last],
+                in_=w1_raw[s][:].rearrange("p j (m t) -> p m j t", t=SLOTS)[:, first:last, :, 2 * u : 2 * u + 2],
             )
 
         def w1_quantize(s, u):
@@ -226,7 +227,8 @@ def tile_picked_pick_mlp_relu2_srt_e_kernel(tc, xT, w1, w2, offs, out):
             first_product(0, 0, t)
 
         w1_interleave(on_vector, 1, 0)
-        w1_interleave(on_scalar, 1, 1)
+        w1_interleave(on_vector, 1, 1, SHARE, P)
+        w1_interleave(on_scalar, 1, 1, 0, SHARE)
         x_quantize(1, 2)
         for u in range(2):
             w1_quantize(1, u)

@@ -13,6 +13,7 @@ U8 = mybir.dt.uint8
 FP8X4 = mybir.dt.float8_e4m3fn_x4
 RELU = mybir.ActivationFunctionType.Relu
 SQUARE = mybir.ActivationFunctionType.Square
+COPY = mybir.ActivationFunctionType.Copy
 MULT = mybir.AluOpType.mult
 
 P = 128
@@ -66,7 +67,7 @@ def tile_picked_pick_mlp_relu2_srt_e_kernel(tc, xT, w1, w2, offs, out):
         x_scales = [tiles("x_scales_first", [P, CH], U8, PASSES), tiles("x_scales_rest", [P, S - CH], U8, PASSES)]
         w1_bf = [
             [
-                keep.tile([P, 2 * P, SLOTS], BF16, name="w1_bf00", tag="shared", align_bytes=ALIGN),
+                keep.tile([P, 2 * P, SLOTS], BF16, name="w1_bf00", align_bytes=ALIGN),
                 keep.tile([P, 2 * P, SLOTS], BF16, name="w1_bf01", align_bytes=ALIGN),
             ],
             tiles("w1_bf1", [P, 2 * P, SLOTS], BF16, 2),
@@ -109,10 +110,13 @@ def tile_picked_pick_mlp_relu2_srt_e_kernel(tc, xT, w1, w2, offs, out):
                 stop=stop,
             )
 
-        def gather(s, j, first=0, last=S):
+        def gather(s, j, first=0, last=S, vector=True):
             window = x[s][j][:, 0 : T - S + last]
             entries = offsets[:, first // PER_COLUMN : last // PER_COLUMN]
-            nc.vector.tensor_copy(picked[s][:, j, first:last], window.indirect(entries))
+            if vector:
+                nc.vector.tensor_copy(picked[s][:, j, first:last], window.indirect(entries))
+            else:
+                nc.scalar.activation(picked[s][:, j, first:last], window.indirect(entries), COPY)
 
         def finish_pass(s):
             for c in range(CHUNKS):
@@ -133,8 +137,8 @@ def tile_picked_pick_mlp_relu2_srt_e_kernel(tc, xT, w1, w2, offs, out):
         def w1_quantize(s, u):
             quantize(w1_codes[s][u][:], w1_scales[s][u][:], w1_bf[s][u][:])
 
-        def w2_interleave(copy, b, i):
-            n = slice(P * i, P * (i + 1))
+        def w2_interleave(copy, b, first, last):
+            n = slice(first, last)
             interleave(copy, w2_bf[b][:, n, :], w2_raw[b][:, :, n])
 
         def w2_quantize(b):
@@ -214,33 +218,34 @@ def tile_picked_pick_mlp_relu2_srt_e_kernel(tc, xT, w1, w2, offs, out):
             x_quantize(0, c)
         gather(1, 1)
         gather(1, 2)
-        finish_pass(1)
+        x_codes[1].append(keep.tile([P, S - CH], U32, name="x_codes_late", align_bytes=ALIGN))
+        for c in range(CHUNKS):
+            gather(1, SLOTS - 1, CH * c, CH * (c + 1), c < 2)
+            interleave((on_scalar, on_vector, on_scalar)[c], x_bf[1][c][:], picked[1][:, :, chunk(c)])
         x_quantize(1, 0)
-
-        for u in range(2):
-            w1_interleave(on_vector, 0, u)
-        for u in range(2):
-            w1_quantize(0, u)
-        x_codes[1].append(keep.tile([P, S - CH], U32, name="x_codes_late", tag="shared", align_bytes=ALIGN))
         x_quantize(1, 1)
+        w1_interleave(on_vector, 0, 0)
+        w1_quantize(0, 0)
+        w1_interleave(on_vector, 0, 1, P - SHARE, P)
+        w1_interleave(on_scalar, 0, 1, 0, P - SHARE)
+        x_quantize(1, 2)
+        w1_quantize(0, 1)
         for t in range(SLOTS):
             first_product(0, 0, t)
-
         w1_interleave(on_vector, 1, 0)
         w1_interleave(on_vector, 1, 1, SHARE, P)
         w1_interleave(on_scalar, 1, 1, 0, SHARE)
-        x_quantize(1, 2)
         for u in range(2):
             w1_quantize(1, u)
         for t in range(SLOTS):
             first_product(0, 1, t)
         for t in range(SLOTS):
-            opening = t // 2
+            opening = min(t, 1)
             first_product(1, opening, t, opening)
             first_product(1, 1 - opening, t, opening)
 
-        for i in range(2):
-            w2_interleave(on_scalar, 0, i)
+        w2_interleave(on_scalar, 0, 0, 160)
+        w2_interleave(on_vector, 0, 160, 256)
         relu(0, 2)
         w2_quantize(0)
         square_vector(0)
@@ -248,7 +253,7 @@ def tile_picked_pick_mlp_relu2_srt_e_kernel(tc, xT, w1, w2, offs, out):
         relu(1, 1)
         h_quantize(0)
         for i in range(2):
-            w2_interleave(on_vector, 1, i)
+            w2_interleave(on_vector, 1, P * i, P * (i + 1))
         square_scalar(1)
         square_vector(1)
         w2_quantize(1)

@@ -24,7 +24,8 @@ CHUNKS = S // CH
 HEAD = T - S + CH
 BANK = 512
 PER_COLUMN = 16
-SHARE = 88
+W1_SCALAR = (40, 88)
+W2_SCALAR = 160
 ALIGN = 64
 
 
@@ -65,13 +66,7 @@ def tile_picked_pick_mlp_relu2_srt_e_kernel(tc, xT, w1, w2, offs, out):
         x_bf = tiles("x_bf", [P, CH, SLOTS], BF16, PASSES, CHUNKS)
         x_codes = [tiles("x_codes_first", [P, CH], U32, PASSES), tiles("x_codes_rest", [P, S - CH], U32, 1)]
         x_scales = [tiles("x_scales_first", [P, CH], U8, PASSES), tiles("x_scales_rest", [P, S - CH], U8, PASSES)]
-        w1_bf = [
-            [
-                keep.tile([P, 2 * P, SLOTS], BF16, name="w1_bf00", align_bytes=ALIGN),
-                keep.tile([P, 2 * P, SLOTS], BF16, name="w1_bf01", align_bytes=ALIGN),
-            ],
-            tiles("w1_bf1", [P, 2 * P, SLOTS], BF16, 2),
-        ]
+        w1_bf = tiles("w1_bf", [P, 2 * P, SLOTS], BF16, PASSES, 2)
         w1_codes = tiles("w1_codes", [P, 2 * P], U32, PASSES, 2)
         w1_scales = tiles("w1_scales", [P, 2 * P], U8, PASSES, 2)
         w2_bf = tiles("w2_bf", [P, N // 2, SLOTS], BF16, 2)
@@ -82,6 +77,7 @@ def tile_picked_pick_mlp_relu2_srt_e_kernel(tc, xT, w1, w2, offs, out):
         h_codes = tiles("h_codes", [P, CH], U32, CHUNKS)
         h_scales = tiles("h_scales", [P, CH], U8, CHUNKS)
         y = tiles("y", [P, 2, CH], F32, CHUNKS, 2)
+        x_codes[1].append(keep.tile([P, S - CH], U32, name="x_codes_late", align_bytes=ALIGN))
 
         on_scalar = nc.scalar.copy
         on_vector = nc.vector.tensor_copy
@@ -118,10 +114,10 @@ def tile_picked_pick_mlp_relu2_srt_e_kernel(tc, xT, w1, w2, offs, out):
             else:
                 nc.scalar.activation(picked[s][:, j, first:last], window.indirect(entries), COPY)
 
-        def finish_pass(s):
+        def finish_pass(s, vector_gathers, vector_rounds):
             for c in range(CHUNKS):
-                gather(s, SLOTS - 1, CH * c, CH * (c + 1))
-                interleave(on_scalar, x_bf[s][c][:], picked[s][:, :, chunk(c)])
+                gather(s, SLOTS - 1, CH * c, CH * (c + 1), c in vector_gathers)
+                interleave(on_vector if c in vector_rounds else on_scalar, x_bf[s][c][:], picked[s][:, :, chunk(c)])
 
         def x_quantize(s, c):
             g = min(c, 1)
@@ -133,6 +129,10 @@ def tile_picked_pick_mlp_relu2_srt_e_kernel(tc, xT, w1, w2, offs, out):
                 out=w1_bf[s][u][:].rearrange("p (t m) j -> p m j t", t=2)[:, first:last],
                 in_=w1_raw[s][:].rearrange("p j (m t) -> p m j t", t=SLOTS)[:, first:last, :, 2 * u : 2 * u + 2],
             )
+
+        def w1_shared_pair(s):
+            w1_interleave(on_vector, s, 1, W1_SCALAR[s], P)
+            w1_interleave(on_scalar, s, 1, 0, W1_SCALAR[s])
 
         def w1_quantize(s, u):
             quantize(w1_codes[s][u][:], w1_scales[s][u][:], w1_bf[s][u][:])
@@ -212,29 +212,26 @@ def tile_picked_pick_mlp_relu2_srt_e_kernel(tc, xT, w1, w2, offs, out):
 
         for j in range(SLOTS - 1):
             gather(0, j)
-        finish_pass(0)
+        finish_pass(0, vector_gathers=(0, 1, 2), vector_rounds=())
         gather(1, 0)
         for c in range(CHUNKS):
             x_quantize(0, c)
         gather(1, 1)
         gather(1, 2)
-        x_codes[1].append(keep.tile([P, S - CH], U32, name="x_codes_late", align_bytes=ALIGN))
-        for c in range(CHUNKS):
-            gather(1, SLOTS - 1, CH * c, CH * (c + 1), c < 2)
-            interleave((on_scalar, on_vector, on_scalar)[c], x_bf[1][c][:], picked[1][:, :, chunk(c)])
+        finish_pass(1, vector_gathers=(0, 1), vector_rounds=(1,))
         x_quantize(1, 0)
         x_quantize(1, 1)
+
         w1_interleave(on_vector, 0, 0)
         w1_quantize(0, 0)
-        w1_interleave(on_vector, 0, 1, P - SHARE, P)
-        w1_interleave(on_scalar, 0, 1, 0, P - SHARE)
+        w1_shared_pair(0)
         x_quantize(1, 2)
         w1_quantize(0, 1)
         for t in range(SLOTS):
             first_product(0, 0, t)
+
         w1_interleave(on_vector, 1, 0)
-        w1_interleave(on_vector, 1, 1, SHARE, P)
-        w1_interleave(on_scalar, 1, 1, 0, SHARE)
+        w1_shared_pair(1)
         for u in range(2):
             w1_quantize(1, u)
         for t in range(SLOTS):
@@ -244,8 +241,8 @@ def tile_picked_pick_mlp_relu2_srt_e_kernel(tc, xT, w1, w2, offs, out):
             first_product(1, opening, t, opening)
             first_product(1, 1 - opening, t, opening)
 
-        w2_interleave(on_scalar, 0, 0, 160)
-        w2_interleave(on_vector, 0, 160, 256)
+        w2_interleave(on_scalar, 0, 0, W2_SCALAR)
+        w2_interleave(on_vector, 0, W2_SCALAR, N // 2)
         relu(0, 2)
         w2_quantize(0)
         square_vector(0)

@@ -27,6 +27,7 @@ PER_COLUMN = 16
 W1_SCALAR = (40, 88)
 W2_SCALAR = 160
 ALIGN = 64
+ROW_ALIGN = 256
 
 
 def tile_picked_pick_mlp_relu2_srt_e_kernel(tc, xT, w1, w2, offs, out):
@@ -41,9 +42,9 @@ def tile_picked_pick_mlp_relu2_srt_e_kernel(tc, xT, w1, w2, offs, out):
         out_view = out.rearrange("(b i p) n -> b p i n", b=2, i=2)
 
         offsets = keep.tile([P, S // PER_COLUMN], U16, name="offsets")
-        x = [[keep.tile([P, T], F32, name="x%d%d" % (s, j)) for j in range(SLOTS)] for s in range(PASSES)]
-        w1_raw = [keep.tile([P, SLOTS, H], F32, name="w1_raw%d" % s) for s in range(PASSES)]
-        w2_raw = [keep.tile([P, SLOTS, N // 2], F32, name="w2_raw%d" % b) for b in range(2)]
+        x = [[keep.tile([P, T], F32, name="x%d%d" % (s, j), align_bytes=ROW_ALIGN) for j in range(SLOTS)] for s in range(PASSES)]
+        w1_raw = [keep.tile([P, SLOTS, H], F32, name="w1_raw%d" % s, align_bytes=ROW_ALIGN) for s in range(PASSES)]
+        w2_raw = [keep.tile([P, SLOTS, N // 2], F32, name="w2_raw%d" % b, align_bytes=ROW_ALIGN) for b in range(2)]
 
         planes = [(s, j) for s in range(PASSES) for j in range(SLOTS)]
         nc.sync.dma_start(x[0][0][:], x_view[0, 0])

@@ -34,7 +34,11 @@ def tile_picked_pick_mlp_relu2_srt_e_kernel(tc, xT, w1, w2, offs, out):
     nc = tc.nc
     with ExitStack() as ctx:
         keep = ctx.enter_context(tc.tile_pool(name="keep", bufs=1))
-        psum = ctx.enter_context(tc.psum_pool(name="psum", bufs=8))
+        psum = ctx.enter_context(tc.psum_pool(name="psum", bufs=1))
+
+        def bank_tile(number):
+            return psum.tile([P, BANK], F32, name="bank%d" % number)
+
 
         x_view = xT.rearrange("(s p j) t -> s j p t", s=PASSES, j=SLOTS)
         w1_view = w1.rearrange("(s p j) c -> s p j c", s=PASSES, j=SLOTS)
@@ -65,20 +69,22 @@ def tile_picked_pick_mlp_relu2_srt_e_kernel(tc, xT, w1, w2, offs, out):
 
         picked = tiles("picked", [P, SLOTS, S], F32, PASSES)
         x_bf = tiles("x_bf", [P, CH, SLOTS], BF16, PASSES, CHUNKS)
-        x_codes = [tiles("x_codes_first", [P, CH], U32, PASSES), tiles("x_codes_rest", [P, S - CH], U32, 1)]
-        x_scales = [tiles("x_scales_first", [P, CH], U8, PASSES), tiles("x_scales_rest", [P, S - CH], U8, PASSES)]
+        x_codes = tiles("x_codes", [P, CH], U32, CHUNKS, PASSES)
+        x_scales = tiles("x_scales", [P, CH], U8, CHUNKS, PASSES)
         w1_bf = tiles("w1_bf", [P, 2 * P, SLOTS], BF16, PASSES, 2)
         w1_codes = tiles("w1_codes", [P, 2 * P], U32, PASSES, 2)
         w1_scales = tiles("w1_scales", [P, 2 * P], U8, PASSES, 2)
         w2_bf = tiles("w2_bf", [P, N // 2, SLOTS], BF16, 2)
-        w2_codes = tiles("w2_codes", [P, N // 2], U32, 2)
+        w2_codes = [
+            keep.tile([P, N // 2], U32, name="w2_codes_first", tag="x_codes_0_1", align_bytes=ALIGN),
+            keep.tile([P, N // 2], U32, name="w2_codes_second", align_bytes=ALIGN),
+        ]
         w2_scales = tiles("w2_scales", [P, N // 2], U8, 2)
         r = tiles("r", [P, SLOTS, CH], F32, CHUNKS)
         h_bf = tiles("h_bf", [P, CH, SLOTS], BF16, CHUNKS)
         h_codes = tiles("h_codes", [P, CH], U32, CHUNKS)
         h_scales = tiles("h_scales", [P, CH], U8, CHUNKS)
         y = tiles("y", [P, 2, CH], F32, CHUNKS, 2)
-        x_codes[1].append(keep.tile([P, S - CH], U32, name="x_codes_late", align_bytes=ALIGN))
 
         on_scalar = nc.scalar.copy
         on_vector = nc.vector.tensor_copy
@@ -121,9 +127,7 @@ def tile_picked_pick_mlp_relu2_srt_e_kernel(tc, xT, w1, w2, offs, out):
                 interleave(on_vector if c in vector_rounds else on_scalar, x_bf[s][c][:], picked[s][:, :, chunk(c)])
 
         def x_quantize(s, c):
-            g = min(c, 1)
-            cols = chunk(c - g)
-            quantize(x_codes[g][s][:, cols], x_scales[g][s][:, cols], x_bf[s][c][:])
+            quantize(x_codes[c][s][:], x_scales[c][s][:], x_bf[s][c][:])
 
         def w1_interleave(copy, s, u, first=0, last=P):
             copy(
@@ -149,7 +153,7 @@ def tile_picked_pick_mlp_relu2_srt_e_kernel(tc, xT, w1, w2, offs, out):
 
         def first_product(g, s, t, opening=0):
             if s == opening:
-                v_banks[g, t] = psum.tile([P, BANK], F32, name="bank")
+                v_banks[g, t] = bank_tile(SLOTS * (g % 2) + t)
             block = slice(P * (t % 2), P * (t % 2 + 1))
             matmul(
                 v_banks[g, t][:, 0 : x_codes[g][s].shape[1]],
@@ -162,25 +166,26 @@ def tile_picked_pick_mlp_relu2_srt_e_kernel(tc, xT, w1, w2, offs, out):
             )
 
         def relu(c, vector_blocks):
-            g = min(c, 1)
             for t in range(SLOTS):
-                v = v_banks[g, t][:, chunk(c - g)]
+                v = v_banks[c, t][:, 0:CH]
                 if t < vector_blocks:
                     nc.vector.tensor_scalar_max(r[c][:, t, :], v, 0.0)
                 else:
                     nc.scalar.activation(r[c][:, t, :], v, RELU)
 
-        def square_views(c, half):
-            n = slice(CH // 2 * half, CH // 2 * (half + 1))
-            return slot_views(h_bf[c][:, n, :], r[c][:, :, n])
+        def relu_block(c, t, vector):
+            v = v_banks[c, t][:, 0:CH]
+            if vector:
+                nc.vector.tensor_scalar_max(r[c][:, t, :], v, 0.0)
+            else:
+                nc.scalar.activation(r[c][:, t, :], v, RELU)
 
-        def square_vector(c):
-            dst, src = square_views(c, 0)
-            nc.vector.tensor_tensor(dst, src, src, MULT)
-
-        def square_scalar(c):
-            dst, src = square_views(c, 1)
-            nc.scalar.activation(dst, src, SQUARE)
+        def square(engine, c, first, last):
+            dst, src = slot_views(h_bf[c][:, first:last, :], r[c][:, :, first:last])
+            if engine is nc.scalar:
+                nc.scalar.activation(dst, src, SQUARE)
+            else:
+                engine.tensor_tensor(dst, src, src, MULT)
 
         def h_quantize(c):
             quantize(h_codes[c][:], h_scales[c][:], h_bf[c][:])
@@ -189,20 +194,20 @@ def tile_picked_pick_mlp_relu2_srt_e_kernel(tc, xT, w1, w2, offs, out):
             block = slice(P * i, P * (i + 1))
             matmul(dst, w2_codes[b][:, block], w2_scales[b][:, block], h_codes[c][:], h_scales[c][:], True, True)
 
-        def product_by_halves(c):
+        def product_by_halves(c, numbers):
             banks = []
             for b in range(2):
-                bank = psum.tile([P, BANK], F32, name="bank")
+                bank = bank_tile(numbers[b])
                 for i in range(2):
                     second_product(bank[:, chunk(i)], c, b, i)
                 banks.append(bank)
             return banks
 
-        def product_by_blocks(c):
+        def product_by_blocks(c, numbers):
             banks = []
             for b in range(2):
                 for i in range(2):
-                    bank = psum.tile([P, BANK], F32, name="bank")
+                    bank = bank_tile(numbers[2 * b + i])
                     second_product(bank[:, 0:CH], c, b, i)
                     banks.append(bank)
             return banks
@@ -228,43 +233,44 @@ def tile_picked_pick_mlp_relu2_srt_e_kernel(tc, xT, w1, w2, offs, out):
         w1_shared_pair(0)
         x_quantize(1, 2)
         w1_quantize(0, 1)
-        for t in range(SLOTS):
-            first_product(0, 0, t)
+        for c in range(2):
+            for t in range(SLOTS):
+                first_product(c, 0, t)
 
         w1_interleave(on_vector, 1, 0)
         w1_shared_pair(1)
         for u in range(2):
             w1_quantize(1, u)
-        for t in range(SLOTS):
-            first_product(0, 1, t)
-        for t in range(SLOTS):
-            opening = min(t, 1)
-            first_product(1, opening, t, opening)
-            first_product(1, 1 - opening, t, opening)
+        for c in range(2):
+            for t in range(SLOTS):
+                first_product(c, 1, t)
 
         w2_interleave(on_scalar, 0, 0, W2_SCALAR)
         w2_interleave(on_vector, 0, W2_SCALAR, N // 2)
         relu(0, 2)
+        for t in range(SLOTS):
+            for s in range(PASSES):
+                first_product(2, s, t)
         w2_quantize(0)
-        square_vector(0)
-        square_scalar(0)
+        square(nc.vector, 0, 0, CH // 2)
+        square(nc.scalar, 0, CH // 2, CH)
         relu(1, 1)
         h_quantize(0)
         for i in range(2):
             w2_interleave(on_vector, 1, P * i, P * (i + 1))
-        square_scalar(1)
-        square_vector(1)
+        square(nc.scalar, 1, CH // 2, CH)
+        square(nc.vector, 1, 0, CH // 2)
         w2_quantize(1)
-        banks_0 = product_by_halves(0)
+        banks_0 = product_by_halves(0, (4, 5))
         relu(2, 0)
         h_quantize(1)
-        banks_1 = product_by_halves(1)
+        banks_1 = product_by_halves(1, (6, 7))
         store_half(on_vector, banks_0[0], 0, 0)
-        square_scalar(2)
-        square_vector(2)
         store_half(on_scalar, banks_0[1], 0, 1)
+        square(nc.scalar, 2, CH // 2, CH)
+        square(nc.vector, 2, 0, CH // 2)
         h_quantize(2)
-        banks_2 = product_by_blocks(2)
+        banks_2 = product_by_blocks(2, (0, 1, 2, 3))
         store_half(on_vector, banks_1[0], 1, 0)
         store_half(on_scalar, banks_1[1], 1, 1)
         for b in range(2):

from contextlib import ExitStack

import concourse.mybir as mybir

K, T, S, H, N = 1024, 2048, 768, 512, 512
FLOPS = 2 * S * (K * H + H * N)

F32 = mybir.dt.float32
BF16 = mybir.dt.bfloat16
U32 = mybir.dt.uint32
U16 = mybir.dt.uint16
U8 = mybir.dt.uint8
FP8X4 = mybir.dt.float8_e4m3fn_x4
RELU = mybir.ActivationFunctionType.Relu
SQUARE = mybir.ActivationFunctionType.Square
COPY = mybir.ActivationFunctionType.Copy
MULT = mybir.AluOpType.mult

P = 128
SLOTS = 4
PASSES = K // (P * SLOTS)
CH = 256
CHUNKS = S // CH
HEAD = T - S + CH
BANK = 512
PER_COLUMN = 16
W1_SCALAR = (40, 88)
W2_SCALAR = 160
ALIGN = 64
ROW_ALIGN = 256


def tile_picked_pick_mlp_relu2_srt_e_kernel(tc, xT, w1, w2, offs, out):
    nc = tc.nc
    with ExitStack() as ctx:
        keep = ctx.enter_context(tc.tile_pool(name="keep", bufs=1))
        psum = ctx.enter_context(tc.psum_pool(name="psum", bufs=1))

        def bank_tile(number):
            return psum.tile([P, BANK], F32, name="bank%d" % number)


        x_view = xT.rearrange("(s p j) t -> s j p t", s=PASSES, j=SLOTS)
        w1_view = w1.rearrange("(s p j) c -> s p j c", s=PASSES, j=SLOTS)
        w2_view = w2.rearrange("(p j) (b c) -> b p j c", j=SLOTS, b=2)
        out_view = out.rearrange("(b i p) n -> b p i n", b=2, i=2)

        offsets = keep.tile([P, S // PER_COLUMN], U16, name="offsets")
        x = [[keep.tile([P, T], F32, name="x%d%d" % (s, j), align_bytes=ROW_ALIGN) for j in range(SLOTS)] for s in range(PASSES)]
        w1_raw = [keep.tile([P, SLOTS, H], F32, name="w1_raw%d" % s, align_bytes=ROW_ALIGN) for s in range(PASSES)]
        w2_raw = [keep.tile([P, SLOTS, N // 2], F32, name="w2_raw%d" % b, align_bytes=ROW_ALIGN) for b in range(2)]

        planes = [(s, j) for s in range(PASSES) for j in range(SLOTS)]
        nc.sync.dma_start(x[0][0][:], x_view[0, 0])
        nc.sync.dma_start(offsets[:], offs)
        for s, j in planes[1:-1]:
            nc.sync.dma_start(x[s][j][:], x_view[s, j])
        for cols in (slice(0, HEAD), slice(HEAD, T)):
            nc.sync.dma_start(x[1][3][:, cols], x_view[1, 3][:, cols])
        for s in range(PASSES):
            nc.sync.dma_start(w1_raw[s][:], w1_view[s])
        for b in range(2):
            nc.sync.dma_start(w2_raw[b][:], w2_view[b])

        def tiles(name, shape, dtype, *counts):
            if len(counts) == 1:
                return [keep.tile(shape, dtype, name="%s_%d" % (name, a), align_bytes=ALIGN) for a in range(counts[0])]
            return [tiles("%s_%d" % (name, a), shape, dtype, *counts[1:]) for a in range(counts[0])]

        picked = tiles("picked", [P, SLOTS, S], F32, PASSES)
        x_bf = tiles("x_bf", [P, CH, SLOTS], BF16, PASSES, CHUNKS)
        x_codes = tiles("x_codes", [P, CH], U32, CHUNKS, PASSES)
        x_scales = tiles("x_scales", [P, CH], U8, CHUNKS, PASSES)
        w1_bf = tiles("w1_bf", [P, 2 * P, SLOTS], BF16, PASSES, 2)
        w1_codes = tiles("w1_codes", [P, 2 * P], U32, PASSES, 2)
        w1_scales = tiles("w1_scales", [P, 2 * P], U8, PASSES, 2)
        w2_bf = tiles("w2_bf", [P, N // 2, SLOTS], BF16, 2)
        w2_codes = [
            keep.tile([P, N // 2], U32, name="w2_codes_first", tag="x_codes_0_1", align_bytes=ALIGN),
            keep.tile([P, N // 2], U32, name="w2_codes_second", align_bytes=ALIGN),
        ]
        w2_scales = tiles("w2_scales", [P, N // 2], U8, 2)
        r = tiles("r", [P, SLOTS, CH], F32, CHUNKS)
        h_bf = tiles("h_bf", [P, CH, SLOTS], BF16, CHUNKS)
        h_codes = tiles("h_codes", [P, CH], U32, CHUNKS)
        h_scales = tiles("h_scales", [P, CH], U8, CHUNKS)
        y = tiles("y", [P, 2, CH], F32, CHUNKS, 2)

        on_scalar = nc.scalar.copy
        on_vector = nc.vector.tensor_copy

        def chunk(c):
            return slice(CH * c, CH * (c + 1))

        def slot_views(dst, src):
            return dst.rearrange("p (c i) t -> p c t i", i=4), src.rearrange("p t (c i) -> p c t i", i=4)

        def interleave(copy, dst, src):
            dst_view, src_view = slot_views(dst, src)
            copy(out=dst_view, in_=src_view)

        def quantize(codes, scales, values):
            nc.vector.quantize_mx(out=codes.bitcast(FP8X4), scales=scales, in_=values.rearrange("p n t -> p (n t)"))

        def matmul(dst, w_codes, w_scales, codes, scales, start, stop):
            nc.tensor.matmul_mx(
                out=dst,
                lhsT=w_codes.bitcast(FP8X4),
                lhsT_scale=w_scales,
                rhs=codes.bitcast(FP8X4),
                rhs_scale=scales,
                start=start,
                stop=stop,
            )

        def gather(s, j, first=0, last=S, vector=True):
            window = x[s][j][:, 0 : T - S + last]
            entries = offsets[:, first // PER_COLUMN : last // PER_COLUMN]
            if vector:
                nc.vector.tensor_copy(picked[s][:, j, first:last], window.indirect(entries))
            else:
                nc.scalar.activation(picked[s][:, j, first:last], window.indirect(entries), COPY)

        def finish_pass(s, vector_gathers, vector_rounds):
            for c in range(CHUNKS):
                gather(s, SLOTS - 1, CH * c, CH * (c + 1), c in vector_gathers)
                interleave(on_vector if c in vector_rounds else on_scalar, x_bf[s][c][:], picked[s][:, :, chunk(c)])

        def x_quantize(s, c):
            quantize(x_codes[c][s][:], x_scales[c][s][:], x_bf[s][c][:])

        def w1_interleave(copy, s, u, first=0, last=P):
            copy(
                out=w1_bf[s][u][:].rearrange("p (t m) j -> p m j t", t=2)[:, first:last],
                in_=w1_raw[s][:].rearrange("p j (m t) -> p m j t", t=SLOTS)[:, first:last, :, 2 * u : 2 * u + 2],
            )

        def w1_shared_pair(s):
            w1_interleave(on_vector, s, 1, W1_SCALAR[s], P)
            w1_interleave(on_scalar, s, 1, 0, W1_SCALAR[s])

        def w1_quantize(s, u):
            quantize(w1_codes[s][u][:], w1_scales[s][u][:], w1_bf[s][u][:])

        def w2_interleave(copy, b, first, last):
            n = slice(first, last)
            interleave(copy, w2_bf[b][:, n, :], w2_raw[b][:, :, n])

        def w2_quantize(b):
            quantize(w2_codes[b][:], w2_scales[b][:], w2_bf[b][:])

        v_banks = {}

        def first_product(g, s, t, opening=0):
            if s == opening:
                v_banks[g, t] = bank_tile(SLOTS * (g % 2) + t)
            block = slice(P * (t % 2), P * (t % 2 + 1))
            matmul(
                v_banks[g, t][:, 0 : x_codes[g][s].shape[1]],
                w1_codes[s][t // 2][:, block],
                w1_scales[s][t // 2][:, block],
                x_codes[g][s][:],
                x_scales[g][s][:],
                start=(s == opening),
                stop=(s != opening),
            )

        def relu(c, vector_blocks):
            for t in range(SLOTS):
                v = v_banks[c, t][:, 0:CH]
                if t < vector_blocks:
                    nc.vector.tensor_scalar_max(r[c][:, t, :], v, 0.0)
                else:
                    nc.scalar.activation(r[c][:, t, :], v, RELU)

        def relu_block(c, t, vector):
            v = v_banks[c, t][:, 0:CH]
            if vector:
                nc.vector.tensor_scalar_max(r[c][:, t, :], v, 0.0)
            else:
                nc.scalar.activation(r[c][:, t, :], v, RELU)

        def square(engine, c, first, last):
            dst, src = slot_views(h_bf[c][:, first:last, :], r[c][:, :, first:last])
            if engine is nc.scalar:
                nc.scalar.activation(dst, src, SQUARE)
            else:
                engine.tensor_tensor(dst, src, src, MULT)

        def h_quantize(c):
            quantize(h_codes[c][:], h_scales[c][:], h_bf[c][:])

        def second_product(dst, c, b, i):
            block = slice(P * i, P * (i + 1))
            matmul(dst, w2_codes[b][:, block], w2_scales[b][:, block], h_codes[c][:], h_scales[c][:], True, True)

        def product_by_halves(c, numbers):
            banks = []
            for b in range(2):
                bank = bank_tile(numbers[b])
                for i in range(2):
                    second_product(bank[:, chunk(i)], c, b, i)
                banks.append(bank)
            return banks

        def product_by_blocks(c, numbers):
            banks = []
            for b in range(2):
                for i in range(2):
                    bank = bank_tile(numbers[2 * b + i])
                    second_product(bank[:, 0:CH], c, b, i)
                    banks.append(bank)
            return banks

        def store_half(copy, bank, c, b):
            copy(out=y[c][b][:].rearrange("p i n -> p (i n)"), in_=bank[:])
            nc.sync.dma_start(out_view[b][:, :, chunk(c)], y[c][b][:])

        for j in range(SLOTS - 1):
            gather(0, j)
        finish_pass(0, vector_gathers=(0, 1, 2), vector_rounds=())
        gather(1, 0)
        for c in range(CHUNKS):
            x_quantize(0, c)
        gather(1, 1)
        gather(1, 2)
        finish_pass(1, vector_gathers=(0, 1), vector_rounds=(1,))
        x_quantize(1, 0)
        x_quantize(1, 1)

        w1_interleave(on_vector, 0, 0)
        w1_quantize(0, 0)
        w1_shared_pair(0)
        x_quantize(1, 2)
        w1_quantize(0, 1)
        for c in range(2):
            for t in range(SLOTS):
                first_product(c, 0, t)

        w1_interleave(on_vector, 1, 0)
        w1_shared_pair(1)
        for u in range(2):
            w1_quantize(1, u)
        for c in range(2):
            for t in range(SLOTS):
                first_product(c, 1, t)

        w2_interleave(on_scalar, 0, 0, W2_SCALAR)
        w2_interleave(on_vector, 0, W2_SCALAR, N // 2)
        relu(0, 2)
        for t in range(SLOTS):
            for s in range(PASSES):
                first_product(2, s, t)
        w2_quantize(0)
        square(nc.vector, 0, 0, CH // 2)
        square(nc.scalar, 0, CH // 2, CH)
        relu(1, 1)
        h_quantize(0)
        for i in range(2):
            w2_interleave(on_vector, 1, P * i, P * (i + 1))
        square(nc.scalar, 1, CH // 2, CH)
        square(nc.vector, 1, 0, CH // 2)
        w2_quantize(1)
        banks_0 = product_by_halves(0, (4, 5))
        relu(2, 0)
        h_quantize(1)
        banks_1 = product_by_halves(1, (6, 7))
        store_half(on_vector, banks_0[0], 0, 0)
        store_half(on_scalar, banks_0[1], 0, 1)
        square(nc.scalar, 2, CH // 2, CH)
        square(nc.vector, 2, 0, CH // 2)
        h_quantize(2)
        banks_2 = product_by_blocks(2, (0, 1, 2, 3))
        store_half(on_vector, banks_1[0], 1, 0)
        store_half(on_scalar, banks_1[1], 1, 1)
        for b in range(2):
            for i in range(2):
                (on_scalar, on_vector)[i](out=y[2][b][:, i, :], in_=banks_2[2 * b + i][:, 0:CH])
                nc.sync.dma_start(out_view[b][:, i, chunk(2)], y[2][b][:, i, :])
